import numpy as np
CORES = [0,1,2,3,4,5,6,7]
N = 8
def setup_inputs(rng):
    return {"x": rng.standard_normal((N, 128, 128), dtype=np.float32)}
def reference(x):
    s = x.min(axis=0)
    return {"y": np.broadcast_to(s, (N,) + s.shape)}

import concourse.bass as bass

RANKS = 8
BLOCKS = 4
COLS = 128 * 128 // BLOCKS // 128

SCRATCH = {
    "xs": ("dram", [BLOCKS, 128, COLS], "float32"),
    "land": ("dram", [RANKS, 128, COLS], "float32"),
    "res": ("dram", [BLOCKS, 128, COLS], "float32"),
}
SEMAPHORES = ["local", "sent", "arrived", "got"]


def rank_program(g, core, T, topo):
    rank = T.rank_of(core)
    if rank is None:
        return
    cores = T.cores
    sem = T.sem

    first = topo.die(cores[0])
    dies = [[r for r in range(RANKS) if topo.die(cores[r]) == first],
            [r for r in range(RANKS) if topo.die(cores[r]) != first]]
    side = 0 if rank in dies[0] else 1
    mine = dies[side].index(rank)
    twin = dies[1 - side][mine]

    def dst_id(r):
        rid, pid, _sengine = topo.addr(cores[r])
        return bass.DstId(rid=rid, pnc=pid)

    g.dma_start(T.xs[:], T.x[:]).then_inc(sem.local, 16)
    g.wait_ge(sem.local, 16)

    copies = []
    for k in range(BLOCKS):
        folders = [f for f in (dies[0][k], dies[1][k]) if f != rank]
        copies.append(bass.RemoteDMATransfer(
            dst_ids=[dst_id(f) for f in folders], dma_engine_mask=0xF << (4 * k), remote_sem=sem.arrived,
            srcs=[T.xs[k]], dsts=[T.land[rank] for _f in folders], alu_op=0))
    g.remote_dma_fused(copies, local_sem=sem.sent)

    g.wait_ge(sem.arrived, 7 * 4)
    takers = [r for r in dies[side] if r != rank] + [twin]
    g.remote_dma_fused(
        [bass.RemoteDMATransfer(
            dst_ids=[dst_id(r) for r in takers], dma_engine_mask=0xFFFF, remote_sem=sem.got,
            srcs=[T.xs[mine]] + [T.land[r] for r in range(RANKS) if r != rank],
            dsts=[T.res[mine] for _r in takers], alu_op=3)],
        local_sem=sem.sent)

    g.wait_ge(sem.got, BLOCKS * 16)
    g.dma_start(T.y[:], T.res[:]).then_inc(sem.local, 16)
    g.wait_ge(sem.local, 32)
    g.wait_ge(sem.sent, 16 + 16)
